import numpy as np
import ml_dtypes


def mxq(x, axis, fmt="e4m3"):
    dtype, down = {"e4m3": (ml_dtypes.float8_e4m3fn, 7), "e5m2": (ml_dtypes.float8_e5m2, 14)}[fmt]
    v = np.moveaxis(np.asarray(x, np.float32).astype(ml_dtypes.bfloat16).astype(np.float64), axis, -1)
    blocks = v.reshape(v.shape[:-1] + (-1, 32))
    amax = np.abs(blocks).max(-1, keepdims=True)
    byte = np.maximum(np.where(amax > 0, np.frexp(amax)[1] - 1 + 127, 0) - down, 1)
    scale = np.exp2(byte - 127.0)
    codes = (blocks / scale).astype(np.float32).astype(dtype).astype(np.float64)
    return np.moveaxis((codes * scale).reshape(v.shape), -1, axis)


WIDE = False


def mx_kscale(k):
    if not WIDE:
        return np.ones(k)
    levels = np.array([10, -10, 5, -5, 0])
    if k % 512:
        return np.exp2(np.random.permutation(np.resize(levels, k // 32))).repeat(32)
    a = np.empty((k // 512, 16))
    for p in range(k // 512):
        a[p, :8] = np.random.permutation(np.resize(levels, 8))
        for g in range(8):
            far = levels[np.abs(levels - a[p, g]) >= 10]
            a[p, g + 8] = far[np.random.randint(len(far))]
    return np.exp2(a.ravel()).repeat(32)


def f64(x):
    return np.asarray(x).astype(np.float64)


def striped(idx):
    return np.tile(idx.reshape(-1, 16).T, (8, 1)).astype(np.uint16)


def unstriped(offs):
    return offs[:16].T.reshape(-1).astype(np.int64)


E2M1 = np.array([0.0, 0.5, 1.0, 1.5, 2.0, 3.0, 4.0, 6.0, -0.0, -0.5, -1.0, -1.5, -2.0, -3.0, -4.0, -6.0])


def pack_weight(w, fmt):
    k, n = w.shape
    w = f64(np.asarray(w, np.float32).astype(ml_dtypes.bfloat16)).reshape(k // 32, 32, n)
    amax = np.abs(w).max(1)
    if fmt == "e4m3":
        byte = np.frexp(amax)[1] - 1 + 127 - 7
    else:
        mant, ex = np.frexp(amax / 6.0)
        byte = np.where(mant > 0.5, ex, ex - 1) + 127
    byte = np.clip(np.where(amax > 0, byte, 1), 1, 254)
    scaled = (w * np.exp2(127.0 - byte)[:, None, :]).reshape(k, n).astype(np.float32)
    by_word = np.ascontiguousarray(scaled.reshape(k // 512, 128, 4, n).transpose(0, 1, 3, 2))
    if fmt == "e4m3":
        words = by_word.astype(ml_dtypes.float8_e4m3fn).view(np.uint8)
    else:
        c = by_word.astype(ml_dtypes.float4_e2m1fn).view(np.uint8) & 0xF
        words = (c[..., 0::2] | (c[..., 1::2] << 4)).reshape(k // 512, 128, 2 * n)
    return np.ascontiguousarray(words), np.ascontiguousarray(byte.astype(np.uint8).reshape(k // 512, 16, n))


def unpack_weight(words, scales, fmt):
    g, _, n = scales.shape
    words = np.ascontiguousarray(words).reshape(g, 128, n, -1)
    if fmt == "e4m3":
        vals = words.view(ml_dtypes.float8_e4m3fn).astype(np.float64)
    else:
        nib = np.empty((g, 128, n, 4), np.uint8)
        nib[..., 0::2] = words & 0xF
        nib[..., 1::2] = words >> 4
        vals = E2M1[nib]
    vals = vals * np.repeat(np.exp2(scales.astype(np.float64) - 127.0), 8, axis=1)[..., None]
    return vals.transpose(0, 1, 3, 2).reshape(g * 512, n)


def pack_table(v):
    words, scales = pack_weight(v, "e4m3")
    return np.concatenate([words.reshape(words.shape[0], -1), scales.reshape(scales.shape[0], -1)], axis=1)


def unpack_table(tab):
    g, t = tab.shape[0], tab.shape[1] // 528
    return unpack_weight(tab[:, :512 * t].reshape(g, 128, t, 4), tab[:, 512 * t:].reshape(g, 16, t), "e4m3")


K, H, M, T, S = 1024, 1536, 128, 4096, 2048


def setup_inputs():
    n = np.random.standard_normal
    s = mx_kscale(K)[:, None]
    u = mx_kscale(H)[:, None]
    w2 = 1.4 * n((H, M)) / np.sqrt(H) / u
    p_w8 = pack_weight(w2[:512], "e4m3")
    p_w4 = pack_weight(w2[512:], "e2m1")
    return {
        "tab": pack_table(n((K, T)) * s),
        "w1": (n((K, H)) / np.sqrt(K) / s * u.T).astype(np.float32),
        "w8_words": p_w8[0],
        "w8_scales": p_w8[1],
        "w4_words": p_w4[0],
        "w4_scales": p_w4[1],
        "offs": striped(np.random.permutation(T)[:S]),
    }


def reference(tab, w1, w8_words, w8_scales, w4_words, w4_scales, offs):
    tab_ = unpack_table(tab)[:, unstriped(offs)]
    w1_ = mxq(f64(w1), 0, "e4m3")
    w8_ = unpack_weight(w8_words, w8_scales, "e4m3")
    w4_ = unpack_weight(w4_words, w4_scales, "e2m1")
    h_ = mxq(np.maximum(w1_.T @ tab_, 0.0), 0, "e4m3")
    y = h_[:512].T @ w8_ + h_[512:].T @ w4_
    return y

@@ -1,0 +1,235 @@
+from contextlib import ExitStack
+
+import concourse.mybir as mybir
+
+K, H, M, T, S = 1024, 1536, 128, 4096, 2048
+FLOPS = 2 * S * H * (K + M)
+
+F32 = mybir.dt.float32
+BF16 = mybir.dt.bfloat16
+I32 = mybir.dt.int32
+U32 = mybir.dt.uint32
+U16 = mybir.dt.uint16
+U8 = mybir.dt.uint8
+E4M3 = mybir.dt.float8_e4m3fn_x4
+E2M1 = mybir.dt.float4_e2m1fn_x4
+RELU = mybir.ActivationFunctionType.Relu
+MAX = mybir.AluOpType.max
+
+P = 128
+PASSES = K // 512
+GROUPS = H // 512
+SLICE = 512
+SLICES = S // SLICE
+EARLY = 2
+
+
+def tile_list_tabmlp_tm_mix_none_kernel(tc, tab, w1, w8_words, w8_scales, w4_words, w4_scales, offs, out):
+    nc = tc.nc
+    with ExitStack() as ctx:
+        keep = ctx.enter_context(tc.tile_pool(name="keep", bufs=1))
+        stage = ctx.enter_context(tc.tile_pool(name="stage", bufs=3))
+        rawpool = ctx.enter_context(tc.tile_pool(name="rawpool", bufs=3))
+        hpool = ctx.enter_context(tc.tile_pool(name="hpool", bufs=5))
+        psum = ctx.enter_context(tc.psum_pool(name="psum", bufs=1))
+
+        offsets = keep.tile([P, S // 16], U16, name="offsets")
+        words = [keep.tile([P, T], I32, name=f"words{a}", align_bytes=64) for a in range(PASSES)]
+        plane = keep.tile([P, T], U8, name="plane", align_bytes=64)
+        raw = {}
+        w1_codes = {(g, a): keep.tile([P, 512], U32, name=f"w1_codes{g}_{a}", align_bytes=64) for g in range(GROUPS) for a in range(PASSES)}
+        w1_scales = {(g, a): keep.tile([P, 512], U8, name=f"w1_scales{g}_{a}", align_bytes=64) for g in range(GROUPS) for a in range(PASSES)}
+        picked = {(a, s): keep.tile([P, SLICE], U32, name=f"picked{a}_{s}", align_bytes=64) for a in range(PASSES) for s in range(SLICES)}
+        picked_scales = [keep.tile([P, SLICE], U8, name=f"picked_scales{s}", align_bytes=64) for s in range(SLICES)]
+        h_codes = {(g, s): keep.tile([P, SLICE], U32, name=f"h_codes{g}_{s}", align_bytes=64) for g in range(GROUPS) for s in range(SLICES)}
+        h_scales = {(g, s): keep.tile([P, SLICE], U8, name=f"h_scales{g}_{s}", align_bytes=64) for g in range(GROUPS) for s in range(SLICES)}
+        dummy = keep.tile([P, 1], F32, name="dummy")
+
+        nc.vector.memset(plane[:, 0 : T // 2].bitcast(I32), 0)
+        nc.gpsimd.memset(plane[:, T // 2 : T].bitcast(I32), 0)
+        nc.vector.memset(dummy[:], 0.0)
+        nc.scalar.activation(dummy[:], dummy[:], RELU)
+        def load_w1(g, a):
+            if (g, a) not in raw:
+                raw[g, a] = rawpool.tile([P, 4, 512], F32, name="raw", align_bytes=64)
+            rows = w1.rearrange("(a p j) c -> a p j c", a=PASSES, p=P, j=4)[a]
+            nc.sync.dma_start(raw[g, a][:], rows[:, :, 512 * g : 512 * (g + 1)])
+
+        def load_words(a):
+            nc.sync.dma_start(words[a][:], tab[a, 0 : 512 * T].rearrange("(p b) -> p b", p=P).bitcast(I32))
+
+        nc.sync.dma_start(offsets[:], offs)
+        load_w1(0, 0)
+        load_words(0)
+        scale_loads = 0
+        for a in range(PASSES):
+            rows = tab[a, 512 * T : 528 * T].rearrange("(Q r t) -> r Q t", Q=4, r=4)
+            for r in range(4):
+                queue = nc.scalar if scale_loads >= 2 else nc.gpsimd
+                queue.dma_start(plane[4 * a + r : P : 32, :].bitcast(I32), rows[r].bitcast(I32))
+                scale_loads += 1
+        raw[0, 1] = rawpool.tile([P, 4, 512], F32, name="raw", align_bytes=64)
+        raw[1, 0] = rawpool.tile([P, 4, 512], F32, name="raw", align_bytes=64)
+        nc.gpsimd.memset(raw[0, 1][:, 0, 0:8], 0.0)
+        nc.gpsimd.memset(words[1][:, 0:8], 0)
+        nc.gpsimd.memset(raw[1, 0][:, 0, 0:8], 0.0)
+        load_w1(0, 1)
+        load_words(1)
+        load_w1(1, 0)
+
+        def load_w2():
+            held = rawpool.tile([P, 11 * M], U8, name="raw", align_bytes=64)
+            nc.gpsimd.memset(held[:, 8 * M : 11 * M].bitcast(I32), 0)
+            nc.sync.dma_start(held[:, 0 : 4 * M].bitcast(I32), w8_words[0].rearrange("p n i -> p (n i)").bitcast(I32))
+            nc.sync.dma_start(
+                held[:, 4 * M : 8 * M].rearrange("p (a b) -> p a b", a=2).bitcast(I32),
+                w4_words.rearrange("a p b -> p a b").bitcast(I32),
+            )
+            w8_rows = w8_scales[0].rearrange("(Q r) n -> r Q n", r=4)
+            w4_rows = w4_scales.rearrange("a (Q r) n -> r Q a n", r=4)
+            for r in range(4):
+                nc.sync.dma_start(held[r:P:32, 8 * M : 9 * M].bitcast(I32), w8_rows[r].bitcast(I32))
+                nc.sync.dma_start(held[r:P:32, 9 * M : 11 * M].rearrange("p (a n) -> p a n", a=2).bitcast(I32), w4_rows[r].bitcast(I32))
+            return held
+
+        def group_w1(g, a, engine):
+            grouped = stage.tile([P, 2048], BF16, name="grouped", align_bytes=64)
+            dst = grouped[:].rearrange("p (t m j) -> p m t j", t=4, j=4)
+            src = raw[g, a][:].rearrange("p j (m t) -> p m t j", t=4)
+            if engine == "scalar":
+                nc.scalar.copy(dst, src)
+            else:
+                nc.vector.tensor_copy(dst, src)
+            return grouped
+
+        def quantize_w1(g, a, grouped):
+            nc.vector.quantize_mx(w1_codes[g, a][:].bitcast(E4M3), w1_scales[g, a][:], grouped[:])
+
+        def gather_words(a, s):
+            nc.vector.tensor_copy(picked[a, s][:], words[a][:].bitcast(U32).indirect(offsets[:, 32 * s : 32 * (s + 1)]))
+
+        def gather_scales(s):
+            nc.vector.tensor_copy(picked_scales[s][:], plane[:].indirect(offsets[:, 32 * s : 32 * (s + 1)]))
+
+        def multiply_1(acc, g, t, a, s, cols, start, stop):
+            nc.tensor.matmul_mx(
+                acc,
+                lhsT=w1_codes[g, a][:, P * t : P * (t + 1)].bitcast(E4M3),
+                lhsT_scale=w1_scales[g, a][:, P * t : P * (t + 1)],
+                rhs=picked[a, s][:, cols].bitcast(E4M3),
+                rhs_scale=picked_scales[s][4 * a :, cols],
+                start=start,
+                stop=stop,
+            )
+
+        def relu_out(dst, src, engine):
+            if engine == "scalar":
+                nc.scalar.activation(dst, src, RELU)
+            else:
+                nc.vector.tensor_scalar(dst, src, 0.0, None, op0=MAX)
+
+        def quantize_h(g, s, h, lo, hi):
+            nc.vector.quantize_mx(h_codes[g, s][:, lo:hi].bitcast(E4M3), h_scales[g, s][:, lo:hi], h[:, 4 * lo : 4 * hi])
+
+        def bank_1():
+            return psum.tile([P, 4, P], F32, name="bank", bufs=6)
+
+        def bank_2():
+            return psum.tile([P, 4, P], F32, name="bank_out", bufs=2)
+
+        quantize_w1(0, 0, group_w1(0, 0, "scalar"))
+        early = {}
+        for s in range(EARLY):
+            gather_scales(s)
+            gather_words(0, s)
+            for t in range(4):
+                bank = bank_1() if len(early) < 6 else bank_2()
+                early[s, t] = bank[:].rearrange("p t n -> p (t n)")
+                multiply_1(early[s, t], 0, t, 0, s, slice(0, SLICE), True, False)
+        quantize_w1(0, 1, group_w1(0, 1, "scalar"))
+        for s in range(EARLY):
+            gather_words(1, s)
+        for s in range(EARLY, SLICES):
+            gather_scales(s)
+            gather_words(0, s)
+        h_rows = {}
+        for s in range(EARLY):
+            h_rows[s] = hpool.tile([P, 4, SLICE], BF16, name="h_rows", bufs=2, align_bytes=64)
+            for t in range(4):
+                multiply_1(early[s, t], 0, t, 1, s, slice(0, SLICE), False, True)
+                relu_out(h_rows[s][:, t, :], early[s, t], "scalar")
+        for s in range(EARLY, SLICES):
+            gather_words(1, s)
+        load_w1(1, 1)
+        for a in range(PASSES):
+            quantize_w1(1, a, group_w1(1, a, "vector"))
+        load_w1(2, 0)
+        load_w1(2, 1)
+
+        def first_layer(g, s, after_block):
+            h = hpool.tile([P, 4 * SLICE], BF16, name="h", align_bytes=64)
+            for b in range(4):
+                cols = slice(P * b, P * (b + 1))
+                bank = bank_1()
+                for t in range(4):
+                    for a in range(PASSES):
+                        multiply_1(bank[:, t, :], g, t, a, s, cols, a == 0, a == PASSES - 1)
+                engine = "vector" if g == 2 and b == 2 else "scalar"
+                relu_out(h[:, 512 * b : 512 * (b + 1)].rearrange("p (n t) -> p n t", t=4), bank[:].rearrange("p t n -> p n t"), engine)
+                after_block(h, b)
+
+        def second_layer(s, tiles):
+            bank = bank_2()
+            for i, b in enumerate(tiles):
+                cols = slice(P * b, P * (b + 1))
+                for g in range(GROUPS):
+                    if g == 0:
+                        weights = w2_codes[:, 0 : 4 * M].bitcast(E4M3)
+                    else:
+                        weights = w2_codes[:, 2 * M * (g + 1) : 2 * M * (g + 2)].bitcast(E2M1)
+                    nc.tensor.matmul_mx(
+                        bank[:, i, :],
+                        lhsT=h_codes[g, s][:, cols].bitcast(E4M3),
+                        lhsT_scale=h_scales[g, s][:, cols],
+                        rhs=weights,
+                        rhs_scale=w2_codes[:, M * (8 + g) : M * (9 + g)],
+                        start=(g == 0),
+                        stop=(g == GROUPS - 1),
+                    )
+            result = stage.tile([P, 4, M], F32, name="result")
+            n = len(tiles)
+            nc.vector.tensor_copy(result[:, 0:n, :], bank[:, 0:n, :])
+            first = SLICE * s + P * tiles[0]
+            nc.sync.dma_start(out[first : first + P * n, :].rearrange("(i p) n -> p i n", p=P), result[:, 0:n, :])
+
+        for g in range(GROUPS):
+            for s in range(SLICES):
+                if g == 0 and s < EARLY:
+                    continue
+
+                def after_block(h, b):
+                    if g < 2:
+                        if b == 3:
+                            quantize_h(g, s, h, 0, SLICE)
+                    elif s < SLICES - 1:
+                        if b % 2 == 1:
+                            quantize_h(g, s, h, P * (b - 1), P * (b + 1))
+                        if b == 3:
+                            second_layer(s, [0, 1, 2, 3])
+                    else:
+                        quantize_h(g, s, h, P * b, P * (b + 1))
+                        if b == 1:
+                            second_layer(s, [0, 1])
+                        elif b > 1:
+                            second_layer(s, [b])
+
+                if g == 1 and s == 0:
+                    for e in range(EARLY):
+                        h = hpool.tile([P, 4 * SLICE], BF16, name="h", align_bytes=64)
+                        nc.vector.tensor_copy(h[:].rearrange("p (n t) -> p n t", t=4), h_rows[e][:].rearrange("p t n -> p n t"))
+                        quantize_h(0, e, h, 0, SLICE)
+                if g == 1 and s == 1:
+                    for a in range(PASSES):
+                        quantize_w1(2, a, group_w1(2, a, "vector"))
+                    w2_codes = load_w2()
+                first_layer(g, s, after_block)

@@ -47,7 +47,7 @@ def tile_list_tabmlp_tm_mix_none_kernel(tc, tab, w1, w8_words, w8_scales, w4_wor
 
         nc.vector.memset(plane[:, 0 : T // 2].bitcast(I32), 0)
         nc.gpsimd.memset(plane[:, T // 2 : T].bitcast(I32), 0)
-        nc.vector.memset(dummy[:], 0.0)
+        nc.gpsimd.memset(dummy[:], 0.0)
         nc.scalar.activation(dummy[:], dummy[:], RELU)
         def load_w1(g, a):
             if (g, a) not in raw:
@@ -70,9 +70,9 @@ def tile_list_tabmlp_tm_mix_none_kernel(tc, tab, w1, w8_words, w8_scales, w4_wor
                 scale_loads += 1
         raw[0, 1] = rawpool.tile([P, 4, 512], F32, name="raw", align_bytes=64)
         raw[1, 0] = rawpool.tile([P, 4, 512], F32, name="raw", align_bytes=64)
-        nc.gpsimd.memset(raw[0, 1][:, 0, 0:8], 0.0)
-        nc.gpsimd.memset(words[1][:, 0:8], 0)
-        nc.gpsimd.memset(raw[1, 0][:, 0, 0:8], 0.0)
+        nc.vector.memset(raw[0, 1][:, 0:2, :], 0.0)
+        nc.vector.memset(words[1][:, 0:8], 0)
+        nc.vector.memset(raw[1, 0][:, 0, 0:8], 0.0)
         load_w1(0, 1)
         load_words(1)
         load_w1(1, 0)
@@ -137,7 +137,7 @@ def tile_list_tabmlp_tm_mix_none_kernel(tc, tab, w1, w8_words, w8_scales, w4_wor
         def bank_2():
             return psum.tile([P, 4, P], F32, name="bank_out", bufs=2)
 
-        quantize_w1(0, 0, group_w1(0, 0, "scalar"))
+        quantize_w1(0, 0, group_w1(0, 0, "vector"))
         early = {}
         for s in range(EARLY):
             gather_scales(s)

from contextlib import ExitStack

import concourse.mybir as mybir

K, H, M, T, S = 1024, 1536, 128, 4096, 2048
FLOPS = 2 * S * H * (K + M)

F32 = mybir.dt.float32
BF16 = mybir.dt.bfloat16
I32 = mybir.dt.int32
U32 = mybir.dt.uint32
U16 = mybir.dt.uint16
U8 = mybir.dt.uint8
E4M3 = mybir.dt.float8_e4m3fn_x4
E2M1 = mybir.dt.float4_e2m1fn_x4
RELU = mybir.ActivationFunctionType.Relu
MAX = mybir.AluOpType.max

P = 128
PASSES = K // 512
GROUPS = H // 512
SLICE = 512
SLICES = S // SLICE
EARLY = 2


def tile_list_tabmlp_tm_mix_none_kernel(tc, tab, w1, w8_words, w8_scales, w4_words, w4_scales, offs, out):
    nc = tc.nc
    with ExitStack() as ctx:
        keep = ctx.enter_context(tc.tile_pool(name="keep", bufs=1))
        stage = ctx.enter_context(tc.tile_pool(name="stage", bufs=3))
        rawpool = ctx.enter_context(tc.tile_pool(name="rawpool", bufs=3))
        hpool = ctx.enter_context(tc.tile_pool(name="hpool", bufs=5))
        psum = ctx.enter_context(tc.psum_pool(name="psum", bufs=1))

        offsets = keep.tile([P, S // 16], U16, name="offsets")
        words = [keep.tile([P, T], I32, name=f"words{a}", align_bytes=64) for a in range(PASSES)]
        plane = keep.tile([P, T], U8, name="plane", align_bytes=64)
        raw = {}
        w1_codes = {(g, a): keep.tile([P, 512], U32, name=f"w1_codes{g}_{a}", align_bytes=64) for g in range(GROUPS) for a in range(PASSES)}
        w1_scales = {(g, a): keep.tile([P, 512], U8, name=f"w1_scales{g}_{a}", align_bytes=64) for g in range(GROUPS) for a in range(PASSES)}
        picked = {(a, s): keep.tile([P, SLICE], U32, name=f"picked{a}_{s}", align_bytes=64) for a in range(PASSES) for s in range(SLICES)}
        picked_scales = [keep.tile([P, SLICE], U8, name=f"picked_scales{s}", align_bytes=64) for s in range(SLICES)]
        h_codes = {(g, s): keep.tile([P, SLICE], U32, name=f"h_codes{g}_{s}", align_bytes=64) for g in range(GROUPS) for s in range(SLICES)}
        h_scales = {(g, s): keep.tile([P, SLICE], U8, name=f"h_scales{g}_{s}", align_bytes=64) for g in range(GROUPS) for s in range(SLICES)}
        dummy = keep.tile([P, 1], F32, name="dummy")

        nc.vector.memset(plane[:, 0 : T // 2].bitcast(I32), 0)
        nc.gpsimd.memset(plane[:, T // 2 : T].bitcast(I32), 0)
        nc.gpsimd.memset(dummy[:], 0.0)
        nc.scalar.activation(dummy[:], dummy[:], RELU)
        def load_w1(g, a):
            if (g, a) not in raw:
                raw[g, a] = rawpool.tile([P, 4, 512], F32, name="raw", align_bytes=64)
            rows = w1.rearrange("(a p j) c -> a p j c", a=PASSES, p=P, j=4)[a]
            nc.sync.dma_start(raw[g, a][:], rows[:, :, 512 * g : 512 * (g + 1)])

        def load_words(a):
            nc.sync.dma_start(words[a][:], tab[a, 0 : 512 * T].rearrange("(p b) -> p b", p=P).bitcast(I32))

        nc.sync.dma_start(offsets[:], offs)
        load_w1(0, 0)
        load_words(0)
        scale_loads = 0
        for a in range(PASSES):
            rows = tab[a, 512 * T : 528 * T].rearrange("(Q r t) -> r Q t", Q=4, r=4)
            for r in range(4):
                queue = nc.scalar if scale_loads >= 2 else nc.gpsimd
                queue.dma_start(plane[4 * a + r : P : 32, :].bitcast(I32), rows[r].bitcast(I32))
                scale_loads += 1
        raw[0, 1] = rawpool.tile([P, 4, 512], F32, name="raw", align_bytes=64)
        raw[1, 0] = rawpool.tile([P, 4, 512], F32, name="raw", align_bytes=64)
        nc.vector.memset(raw[0, 1][:, 0:2, :], 0.0)
        nc.vector.memset(words[1][:, 0:8], 0)
        nc.vector.memset(raw[1, 0][:, 0, 0:8], 0.0)
        load_w1(0, 1)
        load_words(1)
        load_w1(1, 0)

        def load_w2():
            held = rawpool.tile([P, 11 * M], U8, name="raw", align_bytes=64)
            nc.gpsimd.memset(held[:, 8 * M : 11 * M].bitcast(I32), 0)
            nc.sync.dma_start(held[:, 0 : 4 * M].bitcast(I32), w8_words[0].rearrange("p n i -> p (n i)").bitcast(I32))
            nc.sync.dma_start(
                held[:, 4 * M : 8 * M].rearrange("p (a b) -> p a b", a=2).bitcast(I32),
                w4_words.rearrange("a p b -> p a b").bitcast(I32),
            )
            w8_rows = w8_scales[0].rearrange("(Q r) n -> r Q n", r=4)
            w4_rows = w4_scales.rearrange("a (Q r) n -> r Q a n", r=4)
            for r in range(4):
                nc.sync.dma_start(held[r:P:32, 8 * M : 9 * M].bitcast(I32), w8_rows[r].bitcast(I32))
                nc.sync.dma_start(held[r:P:32, 9 * M : 11 * M].rearrange("p (a n) -> p a n", a=2).bitcast(I32), w4_rows[r].bitcast(I32))
            return held

        def group_w1(g, a, engine):
            grouped = stage.tile([P, 2048], BF16, name="grouped", align_bytes=64)
            dst = grouped[:].rearrange("p (t m j) -> p m t j", t=4, j=4)
            src = raw[g, a][:].rearrange("p j (m t) -> p m t j", t=4)
            if engine == "scalar":
                nc.scalar.copy(dst, src)
            else:
                nc.vector.tensor_copy(dst, src)
            return grouped

        def quantize_w1(g, a, grouped):
            nc.vector.quantize_mx(w1_codes[g, a][:].bitcast(E4M3), w1_scales[g, a][:], grouped[:])

        def gather_words(a, s):
            nc.vector.tensor_copy(picked[a, s][:], words[a][:].bitcast(U32).indirect(offsets[:, 32 * s : 32 * (s + 1)]))

        def gather_scales(s):
            nc.vector.tensor_copy(picked_scales[s][:], plane[:].indirect(offsets[:, 32 * s : 32 * (s + 1)]))

        def multiply_1(acc, g, t, a, s, cols, start, stop):
            nc.tensor.matmul_mx(
                acc,
                lhsT=w1_codes[g, a][:, P * t : P * (t + 1)].bitcast(E4M3),
                lhsT_scale=w1_scales[g, a][:, P * t : P * (t + 1)],
                rhs=picked[a, s][:, cols].bitcast(E4M3),
                rhs_scale=picked_scales[s][4 * a :, cols],
                start=start,
                stop=stop,
            )

        def relu_out(dst, src, engine):
            if engine == "scalar":
                nc.scalar.activation(dst, src, RELU)
            else:
                nc.vector.tensor_scalar(dst, src, 0.0, None, op0=MAX)

        def quantize_h(g, s, h, lo, hi):
            nc.vector.quantize_mx(h_codes[g, s][:, lo:hi].bitcast(E4M3), h_scales[g, s][:, lo:hi], h[:, 4 * lo : 4 * hi])

        def bank_1():
            return psum.tile([P, 4, P], F32, name="bank", bufs=6)

        def bank_2():
            return psum.tile([P, 4, P], F32, name="bank_out", bufs=2)

        quantize_w1(0, 0, group_w1(0, 0, "vector"))
        early = {}
        for s in range(EARLY):
            gather_scales(s)
            gather_words(0, s)
            for t in range(4):
                bank = bank_1() if len(early) < 6 else bank_2()
                early[s, t] = bank[:].rearrange("p t n -> p (t n)")
                multiply_1(early[s, t], 0, t, 0, s, slice(0, SLICE), True, False)
        quantize_w1(0, 1, group_w1(0, 1, "scalar"))
        for s in range(EARLY):
            gather_words(1, s)
        for s in range(EARLY, SLICES):
            gather_scales(s)
            gather_words(0, s)
        h_rows = {}
        for s in range(EARLY):
            h_rows[s] = hpool.tile([P, 4, SLICE], BF16, name="h_rows", bufs=2, align_bytes=64)
            for t in range(4):
                multiply_1(early[s, t], 0, t, 1, s, slice(0, SLICE), False, True)
                relu_out(h_rows[s][:, t, :], early[s, t], "scalar")
        for s in range(EARLY, SLICES):
            gather_words(1, s)
        load_w1(1, 1)
        for a in range(PASSES):
            quantize_w1(1, a, group_w1(1, a, "vector"))
        load_w1(2, 0)
        load_w1(2, 1)

        def first_layer(g, s, after_block):
            h = hpool.tile([P, 4 * SLICE], BF16, name="h", align_bytes=64)
            for b in range(4):
                cols = slice(P * b, P * (b + 1))
                bank = bank_1()
                for t in range(4):
                    for a in range(PASSES):
                        multiply_1(bank[:, t, :], g, t, a, s, cols, a == 0, a == PASSES - 1)
                engine = "vector" if g == 2 and b == 2 else "scalar"
                relu_out(h[:, 512 * b : 512 * (b + 1)].rearrange("p (n t) -> p n t", t=4), bank[:].rearrange("p t n -> p n t"), engine)
                after_block(h, b)

        def second_layer(s, tiles):
            bank = bank_2()
            for i, b in enumerate(tiles):
                cols = slice(P * b, P * (b + 1))
                for g in range(GROUPS):
                    if g == 0:
                        weights = w2_codes[:, 0 : 4 * M].bitcast(E4M3)
                    else:
                        weights = w2_codes[:, 2 * M * (g + 1) : 2 * M * (g + 2)].bitcast(E2M1)
                    nc.tensor.matmul_mx(
                        bank[:, i, :],
                        lhsT=h_codes[g, s][:, cols].bitcast(E4M3),
                        lhsT_scale=h_scales[g, s][:, cols],
                        rhs=weights,
                        rhs_scale=w2_codes[:, M * (8 + g) : M * (9 + g)],
                        start=(g == 0),
                        stop=(g == GROUPS - 1),
                    )
            result = stage.tile([P, 4, M], F32, name="result")
            n = len(tiles)
            nc.vector.tensor_copy(result[:, 0:n, :], bank[:, 0:n, :])
            first = SLICE * s + P * tiles[0]
            nc.sync.dma_start(out[first : first + P * n, :].rearrange("(i p) n -> p i n", p=P), result[:, 0:n, :])

        for g in range(GROUPS):
            for s in range(SLICES):
                if g == 0 and s < EARLY:
                    continue

                def after_block(h, b):
                    if g < 2:
                        if b == 3:
                            quantize_h(g, s, h, 0, SLICE)
                    elif s < SLICES - 1:
                        if b % 2 == 1:
                            quantize_h(g, s, h, P * (b - 1), P * (b + 1))
                        if b == 3:
                            second_layer(s, [0, 1, 2, 3])
                    else:
                        quantize_h(g, s, h, P * b, P * (b + 1))
                        if b == 1:
                            second_layer(s, [0, 1])
                        elif b > 1:
                            second_layer(s, [b])

                if g == 1 and s == 0:
                    for e in range(EARLY):
                        h = hpool.tile([P, 4 * SLICE], BF16, name="h", align_bytes=64)
                        nc.vector.tensor_copy(h[:].rearrange("p (n t) -> p n t", t=4), h_rows[e][:].rearrange("p t n -> p n t"))
                        quantize_h(0, e, h, 0, SLICE)
                if g == 1 and s == 1:
                    for a in range(PASSES):
                        quantize_w1(2, a, group_w1(2, a, "vector"))
                    w2_codes = load_w2()
                first_layer(g, s, after_block)
